import numpy as np
import ml_dtypes


def mxq(x, axis, fmt="e4m3"):
    dtype, down = {"e4m3": (ml_dtypes.float8_e4m3fn, 7), "e5m2": (ml_dtypes.float8_e5m2, 14)}[fmt]
    v = np.moveaxis(np.asarray(x, np.float32).astype(ml_dtypes.bfloat16).astype(np.float64), axis, -1)
    blocks = v.reshape(v.shape[:-1] + (-1, 32))
    amax = np.abs(blocks).max(-1, keepdims=True)
    byte = np.maximum(np.where(amax > 0, np.frexp(amax)[1] - 1 + 127, 0) - down, 1)
    scale = np.exp2(byte - 127.0)
    codes = (blocks / scale).astype(np.float32).astype(dtype).astype(np.float64)
    return np.moveaxis((codes * scale).reshape(v.shape), -1, axis)


WIDE = False


def mx_kscale(k):
    if not WIDE:
        return np.ones(k)
    levels = np.array([10, -10, 5, -5, 0])
    if k % 512:
        return np.exp2(np.random.permutation(np.resize(levels, k // 32))).repeat(32)
    a = np.empty((k // 512, 16))
    for p in range(k // 512):
        a[p, :8] = np.random.permutation(np.resize(levels, 8))
        for g in range(8):
            far = levels[np.abs(levels - a[p, g]) >= 10]
            a[p, g + 8] = far[np.random.randint(len(far))]
    return np.exp2(a.ravel()).repeat(32)


BF16 = ml_dtypes.bfloat16


def bf(x):
    return np.asarray(x, np.float32).astype(BF16)


def f64(x):
    return np.asarray(x).astype(np.float64)


E2M1 = np.array([0.0, 0.5, 1.0, 1.5, 2.0, 3.0, 4.0, 6.0, -0.0, -0.5, -1.0, -1.5, -2.0, -3.0, -4.0, -6.0])


def pack_weight(w, fmt):
    k, n = w.shape
    w = f64(bf(w)).reshape(k // 32, 32, n)
    amax = np.abs(w).max(1)
    if fmt == "e4m3":
        byte = np.frexp(amax)[1] - 1 + 127 - 7
    else:
        mant, ex = np.frexp(amax / 6.0)
        byte = np.where(mant > 0.5, ex, ex - 1) + 127
    byte = np.clip(np.where(amax > 0, byte, 1), 1, 254)
    scaled = (w * np.exp2(127.0 - byte)[:, None, :]).reshape(k, n).astype(np.float32)
    by_word = np.ascontiguousarray(scaled.reshape(k // 512, 128, 4, n).transpose(0, 1, 3, 2))
    if fmt == "e4m3":
        words = by_word.astype(ml_dtypes.float8_e4m3fn).view(np.uint8)
    else:
        c = by_word.astype(ml_dtypes.float4_e2m1fn).view(np.uint8) & 0xF
        words = c[..., 0::2] | (c[..., 1::2] << 4)
    return np.ascontiguousarray(words), np.ascontiguousarray(byte.astype(np.uint8).reshape(k // 512, 16, n))


def unpack_weight(words, scales, fmt):
    g, p, n, _ = words.shape
    if fmt == "e4m3":
        vals = np.ascontiguousarray(words).view(ml_dtypes.float8_e4m3fn).astype(np.float64)
    else:
        nib = np.empty((g, p, n, 4), np.uint8)
        nib[..., 0::2] = words & 0xF
        nib[..., 1::2] = words >> 4
        vals = E2M1[nib]
    vals = vals * np.repeat(np.exp2(scales.astype(np.float64) - 127.0), 8, axis=1)[..., None]
    return vals.transpose(0, 1, 3, 2).reshape(g * 512, n)
def pack4(w):
    words, scales = pack_weight(w, "e2m1")
    return words.reshape(words.shape[0], 128, -1), scales


def unpack4(words, scales):
    return unpack_weight(words.reshape(words.shape[0], 128, -1, 2), scales, "e2m1")


def planes(Y):
    n, m = Y.shape
    b = f64(bf(Y)).reshape(n // 32, 32, m)
    amax = np.abs(b).max(1)
    byte = np.clip(np.where(amax > 0, np.frexp(amax)[1] - 1 + 127 - 7, 1), 1, 254)
    codes = (b * np.exp2(127.0 - byte)[:, None, :]).reshape(n, m).astype(np.float32).astype(ml_dtypes.float8_e4m3fn).view(np.uint8)
    words = codes.reshape(n // 512, 128, 4, m).transpose(0, 1, 3, 2)
    return np.ascontiguousarray(words), np.ascontiguousarray(byte.astype(np.uint8).reshape(n // 512, 16, m))


B, L, H, S = 4, 1024, 512, 1024
EPS = 1e-5

def setup_inputs():
    s = mx_kscale(L)
    t = mx_kscale(S)
    amp = np.exp(0.8 * np.random.randn(1, S) + 0.2 * np.random.randn(B, S))
    level = 0.8 * amp * np.random.randn(B, S)
    raw = level + amp * np.random.randn(L, B, S)
    mean = bf(raw.mean(axis=0))
    std = bf(np.sqrt(raw.var(axis=0) + EPS))
    gamma = bf(1 + 0.1 * np.random.randn(S))
    beta = bf(0.3 * np.random.randn(S))
    x = (raw - f64(mean)) / f64(std) * f64(gamma) + f64(beta)
    a = np.random.randn(L, H) / np.sqrt(L)
    x_words, x_scales = pack4(x.reshape(L, B * S) * s[:, None])
    a_words, a_scales = pack4(a / s[:, None])
    bias = bf(0.3 * np.random.randn(H))
    gain = bf((1 + 0.1 * np.random.randn(S)) * t)
    mix = bf(np.random.randn(S, S) / np.sqrt(S) / t[:, None])
    return {"x_words": x_words, "x_scales": x_scales, "a_words": a_words, "a_scales": a_scales,
            "bias": bias, "gain": gain, "mix": mix,
            "gamma": gamma, "beta": beta, "std": std, "mean": mean}

def reference(x_words, x_scales, a_words, a_scales, bias, gain, mix, gamma, beta, std, mean):
    x = unpack4(x_words, x_scales)
    a = unpack4(a_words, a_scales)
    r = (a.T @ x).reshape(H, B, S).transpose(1, 0, 2)
    v = (r + f64(bias)[None, :, None]) * f64(gain)
    z = (mxq(v.reshape(B * H, S), 1, "e4m3") @ mxq(f64(mix), 0, "e4m3")).reshape(B, H, S)
    y = (z - f64(beta)) / f64(gamma) * f64(std)[:, None, :] + f64(mean)[:, None, :]
    Y = y.reshape(B * H, S).T
    words, scales = planes(Y)
    return y, words, scales

@@ -1,0 +1,356 @@
+from contextlib import ExitStack
+
+import concourse.mybir as mybir
+from concourse.masks import make_identity
+
+INST, LOOK, HOR, CH = 4, 1024, 512, 1024
+FLOPS = 2 * INST * HOR * CH * (LOOK + CH)
+
+F32 = mybir.dt.float32
+BF16 = mybir.dt.bfloat16
+I32 = mybir.dt.int32
+U32 = mybir.dt.uint32
+U8 = mybir.dt.uint8
+FP8X4 = mybir.dt.float8_e4m3fn_x4
+FP4X4 = mybir.dt.float4_e2m1fn_x4
+ALU = mybir.AluOpType
+IDENTITY = mybir.ActivationFunctionType.Identity
+
+P = 128
+PACK = 4
+GROUP = P * PACK
+GROUPS = 2
+STEP_TILES = HOR // P
+BANKS = 8
+ALL_STEPS = slice(0, HOR)
+
+
+def tile_revin_horizon_channel_mix_k5_kernel(
+    tc, x_words, x_scales, a_words, a_scales, bias, gain, mix, gamma, beta, std, mean, out_0, out_1, out_2
+):
+    nc = tc.nc
+    with ExitStack() as ctx:
+        keep = ctx.enter_context(tc.tile_pool(name="keep", bufs=1))
+        work = ctx.enter_context(tc.tile_pool(name="work", bufs=2))
+        psum = ctx.enter_context(tc.psum_pool(name="psum", bufs=1))
+        ctx.enter_context(tc.manual_schedule())
+
+        taken = []
+
+        def next_bank(shape):
+            n = len(taken)
+            taken.append(n)
+            return psum.tile(shape, F32, name="bank%d" % n, tag="bank%d" % (n % BANKS))
+
+        a_sc = keep.tile([P, GROUPS, HOR], U8, name="a_sc", align_bytes=64)
+        x_sc_first = keep.tile([P, GROUPS, CH], U8, name="x_sc_first", align_bytes=64)
+        x_sc_rest = keep.tile([P, GROUPS, (INST - 1) * CH], U8, name="x_sc_rest", align_bytes=64)
+        ident = keep.tile([P, P], F32, name="ident")
+        nc.vector.memset(a_sc[:].bitcast(I32), 0)
+        nc.vector.memset(x_sc_first[:].bitcast(I32), 0)
+        nc.vector.memset(x_sc_rest[:].bitcast(I32), 0)
+
+        def load_scales(plane, rows, quads=range(4), queue=nc.sync):
+            for q in quads:
+                queue.dma_start(
+                    out=plane[32 * q : 32 * q + 4].bitcast(I32),
+                    in_=rows[:, 4 * q : 4 * q + 4, :].rearrange("g r n -> r g n").bitcast(I32),
+                )
+
+        x_w = {}
+
+        def load_x(i, g):
+            x_w[i, g] = keep.tile([P, GROUPS, 2 * GROUP], U8, name="x_w%d%d" % (i, g), align_bytes=64)
+            first = 2 * (i * CH + g * GROUP)
+            nc.sync.dma_start(
+                out=x_w[i, g][:].bitcast(I32),
+                in_=x_words[:, :, first : first + 2 * GROUP].rearrange("g p n -> p g n").bitcast(I32),
+            )
+
+        def load_by_word(vec, name, rows, queue=nc.sync):
+            t = keep.tile([P, rows, PACK], BF16, name=name)
+            queue.dma_start(out=t[:], in_=vec)
+            return t
+
+        mix_raw = {}
+
+        def load_mix(g, h):
+            mix_raw[g, h] = keep.tile([P, PACK, GROUP], BF16, name="mix_raw%d%d" % (g, h))
+            nc.sync.dma_start(
+                out=mix_raw[g, h][:],
+                in_=mix[g * GROUP : (g + 1) * GROUP, h * GROUP : (h + 1) * GROUP].rearrange("(p t) n -> p t n", t=PACK),
+            )
+
+        a_w = keep.tile([P, GROUPS, 2 * HOR], U8, name="a_w", align_bytes=64)
+        bias_raw = keep.tile([P, STEP_TILES, 2], BF16, name="bias_raw")
+        gain_col = load_by_word(gain.rearrange("(g p t) -> p g t", g=GROUPS, t=PACK), "gain_col", GROUPS)
+        with nc.allow_non_contiguous_dma(reason="one bias value to a partition"):
+            nc.sync.dma_start(out=bias_raw[:, :, 0:1], in_=bias.rearrange("(s p o) -> p s o", p=P, o=1))
+        load_scales(a_sc, a_scales)
+        nc.sync.dma_start(out=a_w[:].bitcast(I32), in_=a_words.rearrange("g p n -> p g n").bitcast(I32))
+        load_x(0, 0)
+        load_scales(x_sc_first, x_scales[:, :, 0:CH])
+        make_identity(nc, ident[:])
+        load_mix(0, 0)
+        load_x(0, 1)
+        load_mix(1, 0)
+        gamma_col = load_by_word(gamma.rearrange("(h p t) -> p h t", h=GROUPS, t=PACK), "gamma_col", GROUPS)
+        beta_col = load_by_word(beta.rearrange("(h p t) -> p h t", h=GROUPS, t=PACK), "beta_col", GROUPS)
+        std_col = load_by_word(std.rearrange("i (h p t) -> p (i h) t", h=GROUPS, t=PACK), "std_col", INST * GROUPS)
+        mean_col = load_by_word(mean.rearrange("i (h p t) -> p (i h) t", h=GROUPS, t=PACK), "mean_col", INST * GROUPS)
+        load_scales(x_sc_rest, x_scales[:, :, CH:])
+        load_x(1, 0)
+        load_mix(0, 1)
+        load_mix(1, 1)
+        load_x(1, 1)
+        for i in range(2, INST):
+            load_x(i, 0)
+            load_x(i, 1)
+
+        bias_col = keep.tile([P, STEP_TILES], F32, name="bias_col")
+        gain_all = keep.tile([P, GROUPS * 2 * P], F32, name="gain_all")
+        gain_bank = next_bank([P, GROUPS * 2, P])
+        gain_pairs = gain_col[:].rearrange("p g t -> p (g t)").bitcast(F32)
+        for k in range(GROUPS * 2):
+            nc.tensor.transpose(gain_bank[:, k, :], gain_pairs[:, k : k + 1].to_broadcast([P, P]), ident[:])
+        nc.scalar.copy(out=gain_all[:], in_=gain_bank[:].rearrange("p k c -> p (k c)"))
+        nc.scalar.activation(out=bias_col[:], in_=bias_raw[:, :, 0], func=IDENTITY)
+        gain_row = gain_all[:].bitcast(BF16).rearrange("p (g u c e) -> p g u c e", g=GROUPS, u=2, e=2)
+
+        slope = keep.tile([P, INST, GROUPS * PACK], F32, name="slope")
+        offset = keep.tile([P, INST, GROUPS * PACK], F32, name="offset")
+
+        inv_gamma = keep.tile([P, GROUPS * PACK], F32, name="inv_gamma")
+        shift = keep.tile([P, INST, GROUPS * PACK], F32, name="shift")
+        shape = [P, INST, GROUPS * PACK]
+        affine_steps = [
+            lambda: nc.vector.reciprocal(out=inv_gamma[:], in_=gamma_col[:].rearrange("p h t -> p (h t)")),
+            lambda: nc.vector.tensor_tensor(
+                out=slope[:], in0=std_col[:].rearrange("p (i h) t -> p i (h t)", h=GROUPS),
+                in1=inv_gamma[:].unsqueeze(1).to_broadcast(shape), op=ALU.mult,
+            ),
+            lambda: nc.vector.tensor_tensor(
+                out=shift[:], in0=slope[:],
+                in1=beta_col[:].rearrange("p h t -> p (h t)").unsqueeze(1).to_broadcast(shape), op=ALU.mult,
+            ),
+            lambda: nc.vector.tensor_tensor(
+                out=offset[:], in0=mean_col[:].rearrange("p (i h) t -> p i (h t)", h=GROUPS), in1=shift[:],
+                op=ALU.subtract,
+            ),
+        ]
+
+        mix_sorted, mix_q, mix_sc = {}, {}, {}
+
+        def sort_mix(g, h):
+            mix_sorted[g, h] = work.tile([P, PACK * GROUP], BF16, name="mix_sorted%d%d" % (g, h), tag="mix_sorted", bufs=4, align_bytes=64)
+            dst = mix_sorted[g, h][:].rearrange("p (s m t) -> p m t s", s=PACK, t=PACK)
+            src = mix_raw[g, h][:].rearrange("p t (m s) -> p m t s", s=PACK)
+            if g != h:
+                nc.scalar.copy(out=dst, in_=src)
+            else:
+                nc.gpsimd.tensor_scalar(out=dst, in0=src, scalar1=1.0, scalar2=0.0, op0=ALU.mult, op1=ALU.add)
+
+        def quantise_mix(g, h):
+            mix_q[g, h] = keep.tile([P, GROUP], U32, name="mix_q%d%d" % (g, h), align_bytes=64)
+            mix_sc[g, h] = keep.tile([P, GROUP], U8, name="mix_sc%d%d" % (g, h), align_bytes=64)
+            nc.vector.quantize_mx(out=mix_q[g, h][:].bitcast(FP8X4), scales=mix_sc[g, h][:], in_=mix_sorted[g, h][:])
+
+        v_rows, v_cols, v_q, v_sc = {}, {}, {}, {}
+
+        def horizon(i, n):
+            g, s = divmod(n, STEP_TILES)
+            bank = next_bank([P, GROUP])
+            plane, first = (x_sc_first, g * GROUP) if i == 0 else (x_sc_rest, (i - 1) * CH + g * GROUP)
+            for k in range(GROUPS):
+                nc.tensor.matmul_mx(
+                    out=bank[:],
+                    lhsT=a_w[:, k, 2 * P * s : 2 * P * (s + 1)].bitcast(FP4X4),
+                    lhsT_scale=a_sc[:, k, P * s : P * (s + 1)],
+                    rhs=x_w[i, g][:, k, :].bitcast(FP4X4),
+                    rhs_scale=plane[:, k, first : first + GROUP],
+                    start=(k == 0),
+                    stop=(k == GROUPS - 1),
+                )
+            v_rows[i, g, s] = work.tile([P, GROUP], BF16, name="v_rows%d%d%d" % (i, g, s), tag="v_rows", bufs=16)
+            for u in range(2):
+                nc.vector.scalar_tensor_tensor(
+                    out=v_rows[i, g, s][:].rearrange("p (u c e) -> p u c e", u=2, e=2)[:, u],
+                    in0=bank[:].rearrange("p (c u e) -> p u c e", u=2, e=2)[:, u],
+                    scalar=bias_col[:, s : s + 1],
+                    in1=gain_row[:, g, u],
+                    op0=ALU.add,
+                    op1=ALU.mult,
+                )
+
+        def turn_v(i):
+            for g in range(GROUPS):
+                v_cols[i, g] = work.tile([P, HOR * 2], F32, name="v_cols%d%d" % (i, g), tag="v_cols", bufs=3, align_bytes=64)
+                for pair in range(STEP_TILES // 2):
+                    bank = next_bank([P, 2, 2, P])
+                    for k in range(2):
+                        words = v_rows[i, g, 2 * pair + k][:].bitcast(F32)
+                        for u in range(2):
+                            nc.tensor.transpose(bank[:, k, u, :], words[:, u * P : (u + 1) * P], ident[:])
+                    nc.scalar.copy(
+                        out=v_cols[i, g][:, pair * GROUP : (pair + 1) * GROUP].rearrange("p (k j u) -> p k j u", k=2, u=2),
+                        in_=bank[:].rearrange("p k u j -> p k j u"),
+                    )
+
+        def quantise_v(i, g):
+            v_q[i, g] = work.tile([P, HOR], U32, name="v_q%d%d" % (i, g), tag="v_q", bufs=4, align_bytes=64)
+            v_sc[i, g] = work.tile([P, HOR], U8, name="v_sc%d%d" % (i, g), tag="v_sc", bufs=4, align_bytes=64)
+            nc.vector.quantize_mx(out=v_q[i, g][:].bitcast(FP8X4), scales=v_sc[i, g][:], in_=v_cols[i, g][:].bitcast(BF16))
+
+        y_cols, y_bf, y_q = {}, {}, {}
+        y_sc = keep.tile([P, GROUPS, INST * HOR], U8, name="y_sc", align_bytes=64)
+
+        def mix_passes(out, i, h, t, steps):
+            for g in range(GROUPS):
+                nc.tensor.matmul_mx(
+                    out=out,
+                    lhsT=mix_q[g, h][:, P * t : P * (t + 1)].bitcast(FP8X4),
+                    lhsT_scale=mix_sc[g, h][:, P * t : P * (t + 1)],
+                    rhs=v_q[i, g][:, steps].bitcast(FP8X4),
+                    rhs_scale=v_sc[i, g][:, steps],
+                    start=(g == 0),
+                    stop=(g == GROUPS - 1),
+                )
+
+        def denormalise(sums, i, h, t, steps, on_vector):
+            key = (i, h, steps.start)
+            if key not in y_cols:
+                y_cols[key] = work.tile([P, PACK, steps.stop - steps.start], F32, name="y_cols%d%d%d" % key, tag="y_cols", bufs=4)
+            k = h * PACK + t
+            if on_vector:
+                nc.vector.tensor_scalar(
+                    out=y_cols[key][:, t, :], in0=sums, scalar1=slope[:, i, k : k + 1], scalar2=offset[:, i, k : k + 1],
+                    op0=ALU.mult, op1=ALU.add,
+                )
+            else:
+                nc.scalar.activation(
+                    out=y_cols[key][:, t, :], in_=sums, func=IDENTITY,
+                    scale=slope[:, i, k : k + 1], bias=offset[:, i, k : k + 1],
+                )
+
+        def channel_mix(i, h, t, on_vector=False):
+            bank = next_bank([P, HOR])
+            mix_passes(bank[:], i, h, t, ALL_STEPS)
+            denormalise(bank[:], i, h, t, ALL_STEPS, on_vector)
+
+        def channel_mix_half(i, h, steps):
+            for pair in range(2):
+                bank = next_bank([P, 2, HOR // 2])
+                for k in range(2):
+                    mix_passes(bank[:, k, :], i, h, 2 * pair + k, steps)
+                for k in range(2):
+                    denormalise(bank[:, k, :], i, h, 2 * pair + k, steps, pair == 1)
+
+        def round_y(i, h, steps=ALL_STEPS):
+            width = steps.stop - steps.start
+            y_bf[i, h, steps.start] = work.tile([P, width * PACK], BF16, name="y_bf%d%d%d" % (i, h, steps.start), tag="y_bf", align_bytes=64)
+            nc.vector.tensor_copy(
+                out=y_bf[i, h, steps.start][:].rearrange("p (c r t) -> p c t r", r=4, t=PACK),
+                in_=y_cols[i, h, steps.start][:].rearrange("p t (c r) -> p c t r", r=4),
+            )
+
+        def quantise_y(i, h, steps=ALL_STEPS):
+            cols = slice(i * HOR + steps.start, i * HOR + steps.stop)
+            if steps.start == 0:
+                y_q[i, h] = work.tile([P, HOR], U32, name="y_q%d%d" % (i, h), tag="y_q", bufs=3, align_bytes=64)
+            nc.vector.quantize_mx(out=y_q[i, h][:, steps].bitcast(FP8X4), scales=y_sc[:, h, cols], in_=y_bf[i, h, steps.start][:])
+            if steps.stop == HOR:
+                nc.sync.dma_start(
+                    out=out_1[h, :, i * HOR : (i + 1) * HOR, :].rearrange("p m t -> p (m t)").bitcast(I32),
+                    in_=y_q[i, h][:].bitcast(I32),
+                )
+
+        def turn_y_tile(i, h, s, dst, on_vector):
+            bank = next_bank([P, PACK, P])
+            start = HOR // 2 if s >= 2 and (i, h, HOR // 2) in y_cols else 0
+            first = s * P - start
+            for t in range(PACK):
+                nc.tensor.transpose(bank[:, t, :], y_cols[i, h, start][:, t, first : first + P], ident[:])
+            copy = nc.vector.tensor_copy if on_vector else nc.scalar.copy
+            copy(out=dst.rearrange("p (c t) -> p c t", t=PACK), in_=bank[:].rearrange("p t c -> p c t"))
+
+        def turn_y(i, h, on_vector, tiles=range(STEP_TILES), per_store=2):
+            for first in range(tiles.start, tiles.stop, per_store):
+                y_rows = work.tile([P, per_store, GROUP], F32, name="y_rows%d%d%d" % (i, h, first), tag="y_rows", bufs=6)
+                for k in range(per_store):
+                    turn_y_tile(i, h, first + k, y_rows[:, k, :], first + k in on_vector)
+                nc.sync.dma_start(
+                    out=out_0[i, first * P : (first + per_store) * P, h * GROUP : (h + 1) * GROUP].rearrange("(k p) d -> p k d", p=P),
+                    in_=y_rows[:],
+                )
+
+        def store_scales():
+            for q in range(4):
+                nc.sync.dma_start(
+                    out=out_2[:, 4 * q : 4 * q + 4, :].rearrange("h r m -> r h m").bitcast(I32),
+                    in_=y_sc[32 * q : 32 * q + 4].bitcast(I32),
+                )
+
+        sort_mix(0, 0)
+        sort_mix(1, 0)
+        for n in range(8):
+            horizon(0, n)
+            if n >= 4:
+                affine_steps[n - 4]()
+        quantise_mix(0, 0)
+        turn_v(0)
+        quantise_mix(1, 0)
+        quantise_v(0, 0)
+        quantise_v(0, 1)
+        sort_mix(1, 1)
+        horizon(1, 0)
+        horizon(1, 1)
+        for i in range(INST - 1):
+            for t in range(PACK):
+                channel_mix(i, 0, t)
+            if i > 0:
+                round_y(i - 1, 1)
+            horizon(i + 1, 2)
+            if i > 0:
+                quantise_y(i - 1, 1)
+            horizon(i + 1, 3)
+            turn_y(i, 0, (1,) if i > 0 else (1, 3))
+            if i == 0:
+                sort_mix(0, 1)
+                quantise_mix(1, 1)
+            for n in range(4, 8):
+                horizon(i + 1, n)
+            if i == 0:
+                quantise_mix(0, 1)
+            round_y(i, 0)
+            turn_v(i + 1)
+            quantise_v(i + 1, 0)
+            quantise_v(i + 1, 1)
+            quantise_y(i, 0)
+            last = i + 2 == INST
+            for t in range(PACK):
+                channel_mix(i, 1, t, last and t == 3)
+            if not last:
+                horizon(i + 2, 0)
+                horizon(i + 2, 1)
+                turn_y(i, 1, (1,))
+        i = INST - 1
+        early, late = slice(0, HOR // 2), slice(HOR // 2, HOR)
+        channel_mix(i, 0, 0)
+        channel_mix(i, 0, 1)
+        round_y(i - 1, 1)
+        turn_y(i - 1, 1, (2,))
+        quantise_y(i - 1, 1)
+        channel_mix(i, 0, 2)
+        channel_mix(i, 0, 3, True)
+        channel_mix_half(i, 1, early)
+        round_y(i, 0)
+        turn_y(i, 0, ())
+        quantise_y(i, 0)
+        round_y(i, 1, early)
+        channel_mix_half(i, 1, late)
+        quantise_y(i, 1, early)
+        turn_y(i, 1, (), range(0, 2))
+        round_y(i, 1, late)
+        quantise_y(i, 1, late)
+        store_scales()
+        turn_y(i, 1, (3,), range(2, 4), 1)

@@ -145,10 +145,8 @@ def tile_revin_horizon_channel_mix_k5_kernel(
             mix_sorted[g, h] = work.tile([P, PACK * GROUP], BF16, name="mix_sorted%d%d" % (g, h), tag="mix_sorted", bufs=4, align_bytes=64)
             dst = mix_sorted[g, h][:].rearrange("p (s m t) -> p m t s", s=PACK, t=PACK)
             src = mix_raw[g, h][:].rearrange("p t (m s) -> p m t s", s=PACK)
-            if g != h:
-                nc.scalar.copy(out=dst, in_=src)
-            else:
-                nc.gpsimd.tensor_scalar(out=dst, in0=src, scalar1=1.0, scalar2=0.0, op0=ALU.mult, op1=ALU.add)
+            copy = nc.scalar.copy if h == 0 else nc.vector.tensor_copy
+            copy(out=dst, in_=src)
 
         def quantise_mix(g, h):
             mix_q[g, h] = keep.tile([P, GROUP], U32, name="mix_q%d%d" % (g, h), align_bytes=64)
@@ -301,9 +299,9 @@ def tile_revin_horizon_channel_mix_k5_kernel(
         quantise_mix(1, 0)
         quantise_v(0, 0)
         quantise_v(0, 1)
-        sort_mix(1, 1)
         horizon(1, 0)
         horizon(1, 1)
+        sort_mix(0, 1)
         for i in range(INST - 1):
             for t in range(PACK):
                 channel_mix(i, 0, t)
@@ -313,14 +311,14 @@ def tile_revin_horizon_channel_mix_k5_kernel(
             if i > 0:
                 quantise_y(i - 1, 1)
             horizon(i + 1, 3)
-            turn_y(i, 0, (1,) if i > 0 else (1, 3))
             if i == 0:
-                sort_mix(0, 1)
-                quantise_mix(1, 1)
+                sort_mix(1, 1)
+                quantise_mix(0, 1)
+            turn_y(i, 0, (1,) if i > 0 else ())
             for n in range(4, 8):
                 horizon(i + 1, n)
             if i == 0:
-                quantise_mix(0, 1)
+                quantise_mix(1, 1)
             round_y(i, 0)
             turn_v(i + 1)
             quantise_v(i + 1, 0)

@@ -143,9 +143,9 @@ def tile_revin_horizon_channel_mix_k5_kernel(
 
         def sort_mix(g, h):
             mix_sorted[g, h] = work.tile([P, PACK * GROUP], BF16, name="mix_sorted%d%d" % (g, h), tag="mix_sorted", bufs=4, align_bytes=64)
-            dst = mix_sorted[g, h][:].rearrange("p (s m t) -> p m t s", s=PACK, t=PACK)
-            src = mix_raw[g, h][:].rearrange("p t (m s) -> p m t s", s=PACK)
-            copy = nc.scalar.copy if h == 0 else nc.vector.tensor_copy
+            dst = mix_sorted[g, h][:].rearrange("p (s c m t) -> p c s m t", s=PACK, m=2, t=PACK)
+            src = mix_raw[g, h][:].rearrange("p t (c m s) -> p c s m t", m=2, s=PACK)
+            copy = nc.vector.tensor_copy if (g, h) == (0, 1) else nc.scalar.copy
             copy(out=dst, in_=src)
 
         def quantise_mix(g, h):
@@ -303,43 +303,47 @@ def tile_revin_horizon_channel_mix_k5_kernel(
         horizon(1, 1)
         sort_mix(0, 1)
         for i in range(INST - 1):
-            for t in range(PACK):
-                channel_mix(i, 0, t)
-            if i > 0:
-                round_y(i - 1, 1)
+            last = i + 2 == INST
+            channel_mix(i, 0, 0)
+            channel_mix(i, 0, 1)
             horizon(i + 1, 2)
             if i > 0:
-                quantise_y(i - 1, 1)
-            horizon(i + 1, 3)
-            if i == 0:
+                round_y(i - 1, 1)
+            else:
                 sort_mix(1, 1)
+            channel_mix(i, 0, 2)
+            channel_mix(i, 0, 3)
+            horizon(i + 1, 3)
+            if i > 0:
+                quantise_y(i - 1, 1)
+                turn_y(i - 1, 1, ())
+            else:
                 quantise_mix(0, 1)
-            turn_y(i, 0, (1,) if i > 0 else ())
+                quantise_mix(1, 1)
             for n in range(4, 8):
                 horizon(i + 1, n)
-            if i == 0:
-                quantise_mix(1, 1)
+            channel_mix(i, 1, 0)
+            channel_mix(i, 1, 1)
             round_y(i, 0)
             turn_v(i + 1)
             quantise_v(i + 1, 0)
+            channel_mix(i, 1, 2, last)
+            channel_mix(i, 1, 3, last)
             quantise_v(i + 1, 1)
-            quantise_y(i, 0)
-            last = i + 2 == INST
-            for t in range(PACK):
-                channel_mix(i, 1, t, last and t == 3)
             if not last:
                 horizon(i + 2, 0)
                 horizon(i + 2, 1)
-                turn_y(i, 1, (1,))
+            quantise_y(i, 0)
+            turn_y(i, 0, (1,))
         i = INST - 1
         early, late = slice(0, HOR // 2), slice(HOR // 2, HOR)
         channel_mix(i, 0, 0)
-        channel_mix(i, 0, 1)
+        channel_mix(i, 0, 1, True)
         round_y(i - 1, 1)
-        turn_y(i - 1, 1, (2,))
-        quantise_y(i - 1, 1)
         channel_mix(i, 0, 2)
-        channel_mix(i, 0, 3, True)
+        channel_mix(i, 0, 3)
+        turn_y(i - 1, 1, (1,))
+        quantise_y(i - 1, 1)
         channel_mix_half(i, 1, early)
         round_y(i, 0)
         turn_y(i, 0, ())

@@ -46,8 +46,14 @@ def tile_revin_horizon_channel_mix_k5_kernel(
         x_sc_first = keep.tile([P, GROUPS, CH], U8, name="x_sc_first", align_bytes=64)
         x_sc_rest = keep.tile([P, GROUPS, (INST - 1) * CH], U8, name="x_sc_rest", align_bytes=64)
         ident = keep.tile([P, P], F32, name="ident")
+        gain_rows = keep.tile([P, 2 * P], F32, name="gain_rows")
+        bias_rows = keep.tile([P, P], F32, name="bias_rows")
+        norm_rows = keep.tile([P, 2 * P], F32, name="norm_rows")
+        nc.vector.memset(gain_rows[:], 0.0)
         nc.vector.memset(a_sc[:].bitcast(I32), 0)
         nc.vector.memset(x_sc_first[:].bitcast(I32), 0)
+        nc.vector.memset(bias_rows[:], 0.0)
+        nc.vector.memset(norm_rows[:], 0.0)
         nc.vector.memset(x_sc_rest[:].bitcast(I32), 0)
 
         def load_scales(plane, rows, quads=range(4), queue=nc.sync):
@@ -67,10 +73,8 @@ def tile_revin_horizon_channel_mix_k5_kernel(
                 in_=x_words[:, :, first : first + 2 * GROUP].rearrange("g p n -> p g n").bitcast(I32),
             )
 
-        def load_by_word(vec, name, rows, queue=nc.sync):
-            t = keep.tile([P, rows, PACK], BF16, name=name)
-            queue.dma_start(out=t[:], in_=vec)
-            return t
+        def load_rows(dst, first, rows):
+            nc.sync.dma_start(out=dst[first : first + rows.shape[0], :].bitcast(BF16), in_=rows)
 
         mix_raw = {}
 
@@ -82,10 +86,9 @@ def tile_revin_horizon_channel_mix_k5_kernel(
             )
 
         a_w = keep.tile([P, GROUPS, 2 * HOR], U8, name="a_w", align_bytes=64)
-        bias_raw = keep.tile([P, STEP_TILES, 2], BF16, name="bias_raw")
-        gain_col = load_by_word(gain.rearrange("(g p t) -> p g t", g=GROUPS, t=PACK), "gain_col", GROUPS)
-        with nc.allow_non_contiguous_dma(reason="one bias value to a partition"):
-            nc.sync.dma_start(out=bias_raw[:, :, 0:1], in_=bias.rearrange("(s p o) -> p s o", p=P, o=1))
+        bias_raw = keep.tile([STEP_TILES, P], BF16, name="bias_raw")
+        nc.sync.dma_start(out=bias_raw[:], in_=bias.rearrange("(s p) -> s p", p=P))
+        load_rows(gain_rows, 0, gain.rearrange("(g c) -> g c", g=GROUPS))
         load_scales(a_sc, a_scales)
         nc.sync.dma_start(out=a_w[:].bitcast(I32), in_=a_words.rearrange("g p n -> p g n").bitcast(I32))
         load_x(0, 0)
@@ -94,10 +97,10 @@ def tile_revin_horizon_channel_mix_k5_kernel(
         load_mix(0, 0)
         load_x(0, 1)
         load_mix(1, 0)
-        gamma_col = load_by_word(gamma.rearrange("(h p t) -> p h t", h=GROUPS, t=PACK), "gamma_col", GROUPS)
-        beta_col = load_by_word(beta.rearrange("(h p t) -> p h t", h=GROUPS, t=PACK), "beta_col", GROUPS)
-        std_col = load_by_word(std.rearrange("i (h p t) -> p (i h) t", h=GROUPS, t=PACK), "std_col", INST * GROUPS)
-        mean_col = load_by_word(mean.rearrange("i (h p t) -> p (i h) t", h=GROUPS, t=PACK), "mean_col", INST * GROUPS)
+        load_rows(norm_rows, 0, gamma.rearrange("(h d) -> h d", h=GROUPS))
+        load_rows(norm_rows, 2, beta.rearrange("(h d) -> h d", h=GROUPS))
+        load_rows(norm_rows, 4, std.rearrange("i (h d) -> (i h) d", h=GROUPS))
+        load_rows(norm_rows, 12, mean.rearrange("i (h d) -> (i h) d", h=GROUPS))
         load_scales(x_sc_rest, x_scales[:, :, CH:])
         load_x(1, 0)
         load_mix(0, 1)
@@ -107,14 +110,26 @@ def tile_revin_horizon_channel_mix_k5_kernel(
             load_x(i, 0)
             load_x(i, 1)
 
+        def rows_to_columns(rows, count, name):
+            cols = keep.tile([P, count, 2], F32, name=name)
+            bank = next_bank([P, 2, P])
+            for u in range(2):
+                nc.tensor.transpose(bank[:, u, :], rows[:].rearrange("r (p u) -> r u p", u=2)[:, u, :], ident[:])
+            nc.scalar.copy(out=cols[:], in_=bank[:, :, 0:count].rearrange("p u r -> p r u"))
+            return cols
+
+        nc.scalar.activation(out=bias_rows[0:STEP_TILES, :], in_=bias_raw[:], func=IDENTITY)
+        gain_pairs = rows_to_columns(gain_rows, GROUPS, "gain_pairs")
         bias_col = keep.tile([P, STEP_TILES], F32, name="bias_col")
+        bias_bank = next_bank([P, P])
+        nc.tensor.transpose(bias_bank[:], bias_rows[:], ident[:])
+        nc.scalar.copy(out=bias_col[:], in_=bias_bank[:, 0:STEP_TILES])
         gain_all = keep.tile([P, GROUPS * 2 * P], F32, name="gain_all")
-        gain_bank = next_bank([P, GROUPS * 2, P])
-        gain_pairs = gain_col[:].rearrange("p g t -> p (g t)").bitcast(F32)
-        for k in range(GROUPS * 2):
-            nc.tensor.transpose(gain_bank[:, k, :], gain_pairs[:, k : k + 1].to_broadcast([P, P]), ident[:])
-        nc.scalar.copy(out=gain_all[:], in_=gain_bank[:].rearrange("p k c -> p (k c)"))
-        nc.scalar.activation(out=bias_col[:], in_=bias_raw[:, :, 0], func=IDENTITY)
+        gain_bank = next_bank([P, GROUPS, 2, P])
+        for g in range(GROUPS):
+            for u in range(2):
+                nc.tensor.transpose(gain_bank[:, g, u, :], gain_pairs[:, g, u : u + 1].to_broadcast([P, P]), ident[:])
+        nc.scalar.copy(out=gain_all[:], in_=gain_bank[:].rearrange("p g u c -> p (g u c)"))
         gain_row = gain_all[:].bitcast(BF16).rearrange("p (g u c e) -> p g u c e", g=GROUPS, u=2, e=2)
 
         slope = keep.tile([P, INST, GROUPS * PACK], F32, name="slope")
@@ -123,20 +138,23 @@ def tile_revin_horizon_channel_mix_k5_kernel(
         inv_gamma = keep.tile([P, GROUPS * PACK], F32, name="inv_gamma")
         shift = keep.tile([P, INST, GROUPS * PACK], F32, name="shift")
         shape = [P, INST, GROUPS * PACK]
+        norm = {}
+
+        def by_instance(first):
+            return norm["cols"][:, first : first + INST * GROUPS, :].rearrange("p (i h) t -> p i (h t)", h=GROUPS)
+
+        def shared(first):
+            return norm["cols"][:, first : first + GROUPS, :].rearrange("p h t -> p (h t)")
+
         affine_steps = [
-            lambda: nc.vector.reciprocal(out=inv_gamma[:], in_=gamma_col[:].rearrange("p h t -> p (h t)")),
+            lambda: nc.vector.reciprocal(out=inv_gamma[:], in_=shared(0)),
             lambda: nc.vector.tensor_tensor(
-                out=slope[:], in0=std_col[:].rearrange("p (i h) t -> p i (h t)", h=GROUPS),
-                in1=inv_gamma[:].unsqueeze(1).to_broadcast(shape), op=ALU.mult,
+                out=slope[:], in0=by_instance(4), in1=inv_gamma[:].unsqueeze(1).to_broadcast(shape), op=ALU.mult
             ),
             lambda: nc.vector.tensor_tensor(
-                out=shift[:], in0=slope[:],
-                in1=beta_col[:].rearrange("p h t -> p (h t)").unsqueeze(1).to_broadcast(shape), op=ALU.mult,
+                out=shift[:], in0=slope[:], in1=shared(2).unsqueeze(1).to_broadcast(shape), op=ALU.mult
             ),
-            lambda: nc.vector.tensor_tensor(
-                out=offset[:], in0=mean_col[:].rearrange("p (i h) t -> p i (h t)", h=GROUPS), in1=shift[:],
-                op=ALU.subtract,
-            ),
+            lambda: nc.vector.tensor_tensor(out=offset[:], in0=by_instance(12), in1=shift[:], op=ALU.subtract),
         ]
 
         mix_sorted, mix_q, mix_sc = {}, {}, {}
@@ -292,13 +310,16 @@ def tile_revin_horizon_channel_mix_k5_kernel(
         sort_mix(1, 0)
         for n in range(8):
             horizon(0, n)
-            if n >= 4:
-                affine_steps[n - 4]()
+        norm["cols"] = rows_to_columns(norm_rows, 20, "norm_cols")[:].bitcast(BF16)
         quantise_mix(0, 0)
         turn_v(0)
+        affine_steps[0]()
         quantise_mix(1, 0)
+        affine_steps[1]()
         quantise_v(0, 0)
+        affine_steps[2]()
         quantise_v(0, 1)
+        affine_steps[3]()
         horizon(1, 0)
         horizon(1, 1)
         sort_mix(0, 1)

@@ -17,12 +17,20 @@ ALU = mybir.AluOpType
 IDENTITY = mybir.ActivationFunctionType.Identity
 
 P = 128
-PACK = 4
-GROUP = P * PACK
-GROUPS = 2
+SLOTS = 4
+GROUP = P * SLOTS
+LOOK_GROUPS = LOOK // GROUP
+CH_GROUPS = CH // GROUP
 STEP_TILES = HOR // P
+QUADRANTS = 4
+FP4_BYTES = 2
 BANKS = 8
+ALIGN = 64
 ALL_STEPS = slice(0, HOR)
+EARLY_STEPS, LATE_STEPS = slice(0, HOR // 2), slice(HOR // 2, HOR)
+GAMMA_ROW, BETA_ROW, STD_ROW = 0, CH_GROUPS, 2 * CH_GROUPS
+MEAN_ROW = STD_ROW + INST * CH_GROUPS
+NORM_ROWS = MEAN_ROW + INST * CH_GROUPS
 
 
 def tile_revin_horizon_channel_mix_k5_kernel(
@@ -35,20 +43,23 @@ def tile_revin_horizon_channel_mix_k5_kernel(
         psum = ctx.enter_context(tc.psum_pool(name="psum", bufs=1))
         ctx.enter_context(tc.manual_schedule())
 
-        taken = []
+        banks_taken = []
 
         def next_bank(shape):
-            n = len(taken)
-            taken.append(n)
-            return psum.tile(shape, F32, name="bank%d" % n, tag="bank%d" % (n % BANKS))
+            count = len(banks_taken)
+            banks_taken.append(count)
+            return psum.tile(shape, F32, name="bank%d" % count, tag="bank%d" % (count % BANKS))
 
-        a_sc = keep.tile([P, GROUPS, HOR], U8, name="a_sc", align_bytes=64)
-        x_sc_first = keep.tile([P, GROUPS, CH], U8, name="x_sc_first", align_bytes=64)
-        x_sc_rest = keep.tile([P, GROUPS, (INST - 1) * CH], U8, name="x_sc_rest", align_bytes=64)
+        def copy_on(vector):
+            return nc.vector.tensor_copy if vector else nc.scalar.copy
+
+        a_sc = keep.tile([P, LOOK_GROUPS, HOR], U8, name="a_sc", align_bytes=ALIGN)
+        x_sc_first = keep.tile([P, LOOK_GROUPS, CH], U8, name="x_sc_first", align_bytes=ALIGN)
+        x_sc_rest = keep.tile([P, LOOK_GROUPS, (INST - 1) * CH], U8, name="x_sc_rest", align_bytes=ALIGN)
         ident = keep.tile([P, P], F32, name="ident")
-        gain_rows = keep.tile([P, 2 * P], F32, name="gain_rows")
+        gain_rows = keep.tile([P, GROUP // 2], F32, name="gain_rows")
         bias_rows = keep.tile([P, P], F32, name="bias_rows")
-        norm_rows = keep.tile([P, 2 * P], F32, name="norm_rows")
+        norm_rows = keep.tile([P, GROUP // 2], F32, name="norm_rows")
         nc.vector.memset(gain_rows[:], 0.0)
         nc.vector.memset(a_sc[:].bitcast(I32), 0)
         nc.vector.memset(x_sc_first[:].bitcast(I32), 0)
@@ -56,59 +67,59 @@ def tile_revin_horizon_channel_mix_k5_kernel(
         nc.vector.memset(norm_rows[:], 0.0)
         nc.vector.memset(x_sc_rest[:].bitcast(I32), 0)
 
-        def load_scales(plane, rows, quads=range(4), queue=nc.sync):
-            for q in quads:
-                queue.dma_start(
-                    out=plane[32 * q : 32 * q + 4].bitcast(I32),
-                    in_=rows[:, 4 * q : 4 * q + 4, :].rearrange("g r n -> r g n").bitcast(I32),
+        def load_scales(dst, src):
+            for quad in range(QUADRANTS):
+                nc.sync.dma_start(
+                    out=dst[32 * quad : 32 * quad + 4].bitcast(I32),
+                    in_=src[:, 4 * quad : 4 * quad + 4, :].rearrange("n r c -> r n c").bitcast(I32),
                 )
 
         x_w = {}
 
         def load_x(i, g):
-            x_w[i, g] = keep.tile([P, GROUPS, 2 * GROUP], U8, name="x_w%d%d" % (i, g), align_bytes=64)
-            first = 2 * (i * CH + g * GROUP)
+            x_w[i, g] = keep.tile([P, LOOK_GROUPS, FP4_BYTES * GROUP], U8, name="x_w%d%d" % (i, g), align_bytes=ALIGN)
+            byte0 = FP4_BYTES * (i * CH + g * GROUP)
             nc.sync.dma_start(
                 out=x_w[i, g][:].bitcast(I32),
-                in_=x_words[:, :, first : first + 2 * GROUP].rearrange("g p n -> p g n").bitcast(I32),
+                in_=x_words[:, :, byte0 : byte0 + FP4_BYTES * GROUP].rearrange("n p b -> p n b").bitcast(I32),
             )
 
-        def load_rows(dst, first, rows):
-            nc.sync.dma_start(out=dst[first : first + rows.shape[0], :].bitcast(BF16), in_=rows)
+        def load_rows(dst, row0, src):
+            nc.sync.dma_start(out=dst[row0 : row0 + src.shape[0], :].bitcast(BF16), in_=src)
 
         mix_raw = {}
 
         def load_mix(g, h):
-            mix_raw[g, h] = keep.tile([P, PACK, GROUP], BF16, name="mix_raw%d%d" % (g, h))
+            mix_raw[g, h] = keep.tile([P, SLOTS, GROUP], BF16, name="mix_raw%d%d" % (g, h))
             nc.sync.dma_start(
                 out=mix_raw[g, h][:],
-                in_=mix[g * GROUP : (g + 1) * GROUP, h * GROUP : (h + 1) * GROUP].rearrange("(p t) n -> p t n", t=PACK),
+                in_=mix[g * GROUP : (g + 1) * GROUP, h * GROUP : (h + 1) * GROUP].rearrange("(p t) d -> p t d", t=SLOTS),
             )
 
-        a_w = keep.tile([P, GROUPS, 2 * HOR], U8, name="a_w", align_bytes=64)
+        a_w = keep.tile([P, LOOK_GROUPS, FP4_BYTES * HOR], U8, name="a_w", align_bytes=ALIGN)
         bias_raw = keep.tile([STEP_TILES, P], BF16, name="bias_raw")
         nc.sync.dma_start(out=bias_raw[:], in_=bias.rearrange("(s p) -> s p", p=P))
-        load_rows(gain_rows, 0, gain.rearrange("(g c) -> g c", g=GROUPS))
+        load_rows(gain_rows, 0, gain.rearrange("(g c) -> g c", g=CH_GROUPS))
         load_scales(a_sc, a_scales)
-        nc.sync.dma_start(out=a_w[:].bitcast(I32), in_=a_words.rearrange("g p n -> p g n").bitcast(I32))
+        nc.sync.dma_start(out=a_w[:].bitcast(I32), in_=a_words.rearrange("n p b -> p n b").bitcast(I32))
         load_x(0, 0)
         load_scales(x_sc_first, x_scales[:, :, 0:CH])
         make_identity(nc, ident[:])
         load_mix(0, 0)
         load_x(0, 1)
         load_mix(1, 0)
-        load_rows(norm_rows, 0, gamma.rearrange("(h d) -> h d", h=GROUPS))
-        load_rows(norm_rows, 2, beta.rearrange("(h d) -> h d", h=GROUPS))
-        load_rows(norm_rows, 4, std.rearrange("i (h d) -> (i h) d", h=GROUPS))
-        load_rows(norm_rows, 12, mean.rearrange("i (h d) -> (i h) d", h=GROUPS))
+        load_rows(norm_rows, GAMMA_ROW, gamma.rearrange("(h d) -> h d", h=CH_GROUPS))
+        load_rows(norm_rows, BETA_ROW, beta.rearrange("(h d) -> h d", h=CH_GROUPS))
+        load_rows(norm_rows, STD_ROW, std.rearrange("i (h d) -> (i h) d", h=CH_GROUPS))
+        load_rows(norm_rows, MEAN_ROW, mean.rearrange("i (h d) -> (i h) d", h=CH_GROUPS))
         load_scales(x_sc_rest, x_scales[:, :, CH:])
         load_x(1, 0)
         load_mix(0, 1)
         load_mix(1, 1)
         load_x(1, 1)
         for i in range(2, INST):
-            load_x(i, 0)
-            load_x(i, 1)
+            for g in range(CH_GROUPS):
+                load_x(i, g)
 
         def rows_to_columns(rows, count, name):
             cols = keep.tile([P, count, 2], F32, name=name)
@@ -119,134 +130,146 @@ def tile_revin_horizon_channel_mix_k5_kernel(
             return cols
 
         nc.scalar.activation(out=bias_rows[0:STEP_TILES, :], in_=bias_raw[:], func=IDENTITY)
-        gain_pairs = rows_to_columns(gain_rows, GROUPS, "gain_pairs")
+        gain_cols = rows_to_columns(gain_rows, CH_GROUPS, "gain_cols")
         bias_col = keep.tile([P, STEP_TILES], F32, name="bias_col")
         bias_bank = next_bank([P, P])
         nc.tensor.transpose(bias_bank[:], bias_rows[:], ident[:])
         nc.scalar.copy(out=bias_col[:], in_=bias_bank[:, 0:STEP_TILES])
-        gain_all = keep.tile([P, GROUPS * 2 * P], F32, name="gain_all")
-        gain_bank = next_bank([P, GROUPS, 2, P])
-        for g in range(GROUPS):
+        gain_words = keep.tile([P, CH // 2], F32, name="gain_words")
+        gain_bank = next_bank([P, CH_GROUPS, 2, P])
+        for g in range(CH_GROUPS):
             for u in range(2):
-                nc.tensor.transpose(gain_bank[:, g, u, :], gain_pairs[:, g, u : u + 1].to_broadcast([P, P]), ident[:])
-        nc.scalar.copy(out=gain_all[:], in_=gain_bank[:].rearrange("p g u c -> p (g u c)"))
-        gain_row = gain_all[:].bitcast(BF16).rearrange("p (g u c e) -> p g u c e", g=GROUPS, u=2, e=2)
+                nc.tensor.transpose(gain_bank[:, g, u, :], gain_cols[:, g, u : u + 1].to_broadcast([P, P]), ident[:])
+        nc.scalar.copy(out=gain_words[:], in_=gain_bank[:].rearrange("p g u w -> p (g u w)"))
+        gain_spread = gain_words[:].bitcast(BF16).rearrange("p (g u w e) -> p g u w e", g=CH_GROUPS, u=2, e=2)
 
-        slope = keep.tile([P, INST, GROUPS * PACK], F32, name="slope")
-        offset = keep.tile([P, INST, GROUPS * PACK], F32, name="offset")
+        affine_shape = [P, INST, CH_GROUPS * SLOTS]
+        slope = keep.tile(affine_shape, F32, name="slope")
+        offset = keep.tile(affine_shape, F32, name="offset")
+        inv_gamma = keep.tile([P, CH_GROUPS * SLOTS], F32, name="inv_gamma")
+        beta_slope = keep.tile(affine_shape, F32, name="beta_slope")
 
-        inv_gamma = keep.tile([P, GROUPS * PACK], F32, name="inv_gamma")
-        shift = keep.tile([P, INST, GROUPS * PACK], F32, name="shift")
-        shape = [P, INST, GROUPS * PACK]
-        norm = {}
+        def affine_steps(norm_cols):
+            def per_instance(row0):
+                return norm_cols[:, row0 : row0 + INST * CH_GROUPS, :].rearrange("p (i h) t -> p i (h t)", h=CH_GROUPS)
 
-        def by_instance(first):
-            return norm["cols"][:, first : first + INST * GROUPS, :].rearrange("p (i h) t -> p i (h t)", h=GROUPS)
+            def shared(row0):
+                return norm_cols[:, row0 : row0 + CH_GROUPS, :].rearrange("p h t -> p (h t)")
 
-        def shared(first):
-            return norm["cols"][:, first : first + GROUPS, :].rearrange("p h t -> p (h t)")
-
-        affine_steps = [
-            lambda: nc.vector.reciprocal(out=inv_gamma[:], in_=shared(0)),
-            lambda: nc.vector.tensor_tensor(
-                out=slope[:], in0=by_instance(4), in1=inv_gamma[:].unsqueeze(1).to_broadcast(shape), op=ALU.mult
-            ),
-            lambda: nc.vector.tensor_tensor(
-                out=shift[:], in0=slope[:], in1=shared(2).unsqueeze(1).to_broadcast(shape), op=ALU.mult
-            ),
-            lambda: nc.vector.tensor_tensor(out=offset[:], in0=by_instance(12), in1=shift[:], op=ALU.subtract),
-        ]
+            return [
+                lambda: nc.vector.reciprocal(out=inv_gamma[:], in_=shared(GAMMA_ROW)),
+                lambda: nc.vector.tensor_tensor(
+                    out=slope[:],
+                    in0=per_instance(STD_ROW),
+                    in1=inv_gamma[:].unsqueeze(1).to_broadcast(affine_shape),
+                    op=ALU.mult,
+                ),
+                lambda: nc.vector.tensor_tensor(
+                    out=beta_slope[:],
+                    in0=slope[:],
+                    in1=shared(BETA_ROW).unsqueeze(1).to_broadcast(affine_shape),
+                    op=ALU.mult,
+                ),
+                lambda: nc.vector.tensor_tensor(
+                    out=offset[:], in0=per_instance(MEAN_ROW), in1=beta_slope[:], op=ALU.subtract
+                ),
+            ]
 
         mix_sorted, mix_q, mix_sc = {}, {}, {}
 
-        def sort_mix(g, h):
-            mix_sorted[g, h] = work.tile([P, PACK * GROUP], BF16, name="mix_sorted%d%d" % (g, h), tag="mix_sorted", bufs=4, align_bytes=64)
-            dst = mix_sorted[g, h][:].rearrange("p (s c m t) -> p c s m t", s=PACK, m=2, t=PACK)
-            src = mix_raw[g, h][:].rearrange("p t (c m s) -> p c s m t", m=2, s=PACK)
-            copy = nc.vector.tensor_copy if (g, h) == (0, 1) else nc.scalar.copy
-            copy(out=dst, in_=src)
+        def sort_mix(g, h, on_vector=False):
+            mix_sorted[g, h] = work.tile(
+                [P, SLOTS * GROUP], BF16, name="mix_sorted%d%d" % (g, h), tag="mix_sorted", bufs=4, align_bytes=ALIGN
+            )
+            copy_on(on_vector)(
+                out=mix_sorted[g, h][:].rearrange("p (o b m t) -> p b o m t", o=SLOTS, m=2, t=SLOTS),
+                in_=mix_raw[g, h][:].rearrange("p t (b m o) -> p b o m t", m=2, o=SLOTS),
+            )
 
         def quantise_mix(g, h):
-            mix_q[g, h] = keep.tile([P, GROUP], U32, name="mix_q%d%d" % (g, h), align_bytes=64)
-            mix_sc[g, h] = keep.tile([P, GROUP], U8, name="mix_sc%d%d" % (g, h), align_bytes=64)
+            mix_q[g, h] = keep.tile([P, GROUP], U32, name="mix_q%d%d" % (g, h), align_bytes=ALIGN)
+            mix_sc[g, h] = keep.tile([P, GROUP], U8, name="mix_sc%d%d" % (g, h), align_bytes=ALIGN)
             nc.vector.quantize_mx(out=mix_q[g, h][:].bitcast(FP8X4), scales=mix_sc[g, h][:], in_=mix_sorted[g, h][:])
 
         v_rows, v_cols, v_q, v_sc = {}, {}, {}, {}
 
-        def horizon(i, n):
-            g, s = divmod(n, STEP_TILES)
+        def horizon(i, part):
+            g, s = divmod(part, STEP_TILES)
             bank = next_bank([P, GROUP])
-            plane, first = (x_sc_first, g * GROUP) if i == 0 else (x_sc_rest, (i - 1) * CH + g * GROUP)
-            for k in range(GROUPS):
+            x_sc, col0 = (x_sc_first, g * GROUP) if i == 0 else (x_sc_rest, (i - 1) * CH + g * GROUP)
+            for n in range(LOOK_GROUPS):
                 nc.tensor.matmul_mx(
                     out=bank[:],
-                    lhsT=a_w[:, k, 2 * P * s : 2 * P * (s + 1)].bitcast(FP4X4),
-                    lhsT_scale=a_sc[:, k, P * s : P * (s + 1)],
-                    rhs=x_w[i, g][:, k, :].bitcast(FP4X4),
-                    rhs_scale=plane[:, k, first : first + GROUP],
-                    start=(k == 0),
-                    stop=(k == GROUPS - 1),
+                    lhsT=a_w[:, n, FP4_BYTES * P * s : FP4_BYTES * P * (s + 1)].bitcast(FP4X4),
+                    lhsT_scale=a_sc[:, n, P * s : P * (s + 1)],
+                    rhs=x_w[i, g][:, n, :].bitcast(FP4X4),
+                    rhs_scale=x_sc[:, n, col0 : col0 + GROUP],
+                    start=(n == 0),
+                    stop=(n == LOOK_GROUPS - 1),
                 )
             v_rows[i, g, s] = work.tile([P, GROUP], BF16, name="v_rows%d%d%d" % (i, g, s), tag="v_rows", bufs=16)
             for u in range(2):
                 nc.vector.scalar_tensor_tensor(
-                    out=v_rows[i, g, s][:].rearrange("p (u c e) -> p u c e", u=2, e=2)[:, u],
-                    in0=bank[:].rearrange("p (c u e) -> p u c e", u=2, e=2)[:, u],
+                    out=v_rows[i, g, s][:].rearrange("p (u w e) -> p u w e", u=2, e=2)[:, u],
+                    in0=bank[:].rearrange("p (w u e) -> p u w e", u=2, e=2)[:, u],
                     scalar=bias_col[:, s : s + 1],
-                    in1=gain_row[:, g, u],
+                    in1=gain_spread[:, g, u],
                     op0=ALU.add,
                     op1=ALU.mult,
                 )
 
-        def turn_v(i):
-            for g in range(GROUPS):
-                v_cols[i, g] = work.tile([P, HOR * 2], F32, name="v_cols%d%d" % (i, g), tag="v_cols", bufs=3, align_bytes=64)
-                for pair in range(STEP_TILES // 2):
+        def turn_v(i, shared_copies=False):
+            for g in range(CH_GROUPS):
+                v_cols[i, g] = work.tile(
+                    [P, HOR * 2], F32, name="v_cols%d%d" % (i, g), tag="v_cols", bufs=3, align_bytes=ALIGN
+                )
+                for half in range(2):
                     bank = next_bank([P, 2, 2, P])
                     for k in range(2):
-                        words = v_rows[i, g, 2 * pair + k][:].bitcast(F32)
+                        words = v_rows[i, g, 2 * half + k][:].bitcast(F32)
                         for u in range(2):
                             nc.tensor.transpose(bank[:, k, u, :], words[:, u * P : (u + 1) * P], ident[:])
-                    nc.scalar.copy(
-                        out=v_cols[i, g][:, pair * GROUP : (pair + 1) * GROUP].rearrange("p (k j u) -> p k j u", k=2, u=2),
+                    copy_on(shared_copies and half == 1)(
+                        out=v_cols[i, g][:, half * HOR : (half + 1) * HOR].rearrange("p (k j u) -> p k j u", k=2, u=2),
                         in_=bank[:].rearrange("p k u j -> p k j u"),
                     )
 
         def quantise_v(i, g):
-            v_q[i, g] = work.tile([P, HOR], U32, name="v_q%d%d" % (i, g), tag="v_q", bufs=4, align_bytes=64)
-            v_sc[i, g] = work.tile([P, HOR], U8, name="v_sc%d%d" % (i, g), tag="v_sc", bufs=4, align_bytes=64)
-            nc.vector.quantize_mx(out=v_q[i, g][:].bitcast(FP8X4), scales=v_sc[i, g][:], in_=v_cols[i, g][:].bitcast(BF16))
+            v_q[i, g] = work.tile([P, HOR], U32, name="v_q%d%d" % (i, g), tag="v_q", bufs=4, align_bytes=ALIGN)
+            v_sc[i, g] = work.tile([P, HOR], U8, name="v_sc%d%d" % (i, g), tag="v_sc", bufs=4, align_bytes=ALIGN)
+            nc.vector.quantize_mx(
+                out=v_q[i, g][:].bitcast(FP8X4), scales=v_sc[i, g][:], in_=v_cols[i, g][:].bitcast(BF16)
+            )
 
         y_cols, y_bf, y_q = {}, {}, {}
-        y_sc = keep.tile([P, GROUPS, INST * HOR], U8, name="y_sc", align_bytes=64)
+        y_sc = [keep.tile([P, CH_GROUPS, HOR], U8, name="y_sc%d" % i, align_bytes=ALIGN) for i in range(INST)]
 
-        def mix_passes(out, i, h, t, steps):
-            for g in range(GROUPS):
+        def mix_passes(sums, i, h, t, steps):
+            for g in range(CH_GROUPS):
                 nc.tensor.matmul_mx(
-                    out=out,
+                    out=sums,
                     lhsT=mix_q[g, h][:, P * t : P * (t + 1)].bitcast(FP8X4),
                     lhsT_scale=mix_sc[g, h][:, P * t : P * (t + 1)],
                     rhs=v_q[i, g][:, steps].bitcast(FP8X4),
                     rhs_scale=v_sc[i, g][:, steps],
                     start=(g == 0),
-                    stop=(g == GROUPS - 1),
+                    stop=(g == CH_GROUPS - 1),
                 )
 
         def denormalise(sums, i, h, t, steps, on_vector):
             key = (i, h, steps.start)
             if key not in y_cols:
-                y_cols[key] = work.tile([P, PACK, steps.stop - steps.start], F32, name="y_cols%d%d%d" % key, tag="y_cols", bufs=4)
-            k = h * PACK + t
+                y_cols[key] = work.tile(
+                    [P, SLOTS, steps.stop - steps.start], F32, name="y_cols%d%d%d" % key, tag="y_cols", bufs=4
+                )
+            slope_col = slope[:, i, h * SLOTS + t : h * SLOTS + t + 1]
+            offset_col = offset[:, i, h * SLOTS + t : h * SLOTS + t + 1]
             if on_vector:
                 nc.vector.tensor_scalar(
-                    out=y_cols[key][:, t, :], in0=sums, scalar1=slope[:, i, k : k + 1], scalar2=offset[:, i, k : k + 1],
-                    op0=ALU.mult, op1=ALU.add,
+                    out=y_cols[key][:, t, :], in0=sums, scalar1=slope_col, scalar2=offset_col, op0=ALU.mult, op1=ALU.add
                 )
             else:
-                nc.scalar.activation(
-                    out=y_cols[key][:, t, :], in_=sums, func=IDENTITY,
-                    scale=slope[:, i, k : k + 1], bias=offset[:, i, k : k + 1],
-                )
+                nc.scalar.activation(out=y_cols[key][:, t, :], in_=sums, func=IDENTITY, scale=slope_col, bias=offset_col)
 
         def channel_mix(i, h, t, on_vector=False):
             bank = next_bank([P, HOR])
@@ -254,77 +277,71 @@ def tile_revin_horizon_channel_mix_k5_kernel(
             denormalise(bank[:], i, h, t, ALL_STEPS, on_vector)
 
         def channel_mix_half(i, h, steps):
-            for pair in range(2):
+            for t0 in (0, 2):
                 bank = next_bank([P, 2, HOR // 2])
                 for k in range(2):
-                    mix_passes(bank[:, k, :], i, h, 2 * pair + k, steps)
+                    mix_passes(bank[:, k, :], i, h, t0 + k, steps)
                 for k in range(2):
-                    denormalise(bank[:, k, :], i, h, 2 * pair + k, steps, pair == 1)
+                    denormalise(bank[:, k, :], i, h, t0 + k, steps, on_vector=(t0 == 2))
 
         def round_y(i, h, steps=ALL_STEPS):
-            width = steps.stop - steps.start
-            y_bf[i, h, steps.start] = work.tile([P, width * PACK], BF16, name="y_bf%d%d%d" % (i, h, steps.start), tag="y_bf", align_bytes=64)
+            key = (i, h, steps.start)
+            y_bf[key] = work.tile(
+                [P, (steps.stop - steps.start) * SLOTS], BF16, name="y_bf%d%d%d" % key, tag="y_bf", align_bytes=ALIGN
+            )
             nc.vector.tensor_copy(
-                out=y_bf[i, h, steps.start][:].rearrange("p (c r t) -> p c t r", r=4, t=PACK),
-                in_=y_cols[i, h, steps.start][:].rearrange("p t (c r) -> p c t r", r=4),
+                out=y_bf[key][:].rearrange("p (b r t) -> p b t r", r=4, t=SLOTS),
+                in_=y_cols[key][:].rearrange("p t (b r) -> p b t r", r=4),
             )
 
         def quantise_y(i, h, steps=ALL_STEPS):
-            cols = slice(i * HOR + steps.start, i * HOR + steps.stop)
             if steps.start == 0:
-                y_q[i, h] = work.tile([P, HOR], U32, name="y_q%d%d" % (i, h), tag="y_q", bufs=3, align_bytes=64)
-            nc.vector.quantize_mx(out=y_q[i, h][:, steps].bitcast(FP8X4), scales=y_sc[:, h, cols], in_=y_bf[i, h, steps.start][:])
+                y_q[i, h] = work.tile([P, HOR], U32, name="y_q%d%d" % (i, h), tag="y_q", bufs=3, align_bytes=ALIGN)
+            nc.vector.quantize_mx(
+                out=y_q[i, h][:, steps].bitcast(FP8X4), scales=y_sc[i][:, h, steps], in_=y_bf[i, h, steps.start][:]
+            )
             if steps.stop == HOR:
                 nc.sync.dma_start(
-                    out=out_1[h, :, i * HOR : (i + 1) * HOR, :].rearrange("p m t -> p (m t)").bitcast(I32),
+                    out=out_1[h, :, i * HOR : (i + 1) * HOR, :].rearrange("p j t -> p (j t)").bitcast(I32),
                     in_=y_q[i, h][:].bitcast(I32),
                 )
 
-        def turn_y_tile(i, h, s, dst, on_vector):
-            bank = next_bank([P, PACK, P])
-            start = HOR // 2 if s >= 2 and (i, h, HOR // 2) in y_cols else 0
-            first = s * P - start
-            for t in range(PACK):
-                nc.tensor.transpose(bank[:, t, :], y_cols[i, h, start][:, t, first : first + P], ident[:])
-            copy = nc.vector.tensor_copy if on_vector else nc.scalar.copy
-            copy(out=dst.rearrange("p (c t) -> p c t", t=PACK), in_=bank[:].rearrange("p t c -> p c t"))
-
-        def turn_y(i, h, on_vector, tiles=range(STEP_TILES), per_store=2):
-            for first in range(tiles.start, tiles.stop, per_store):
-                y_rows = work.tile([P, per_store, GROUP], F32, name="y_rows%d%d%d" % (i, h, first), tag="y_rows", bufs=6)
-                for k in range(per_store):
-                    turn_y_tile(i, h, first + k, y_rows[:, k, :], first + k in on_vector)
+        def store_scales(i):
+            for quad in range(QUADRANTS):
                 nc.sync.dma_start(
-                    out=out_0[i, first * P : (first + per_store) * P, h * GROUP : (h + 1) * GROUP].rearrange("(k p) d -> p k d", p=P),
+                    out=out_2[:, 4 * quad : 4 * quad + 4, i * HOR : (i + 1) * HOR].rearrange("h r j -> r h j").bitcast(I32),
+                    in_=y_sc[i][32 * quad : 32 * quad + 4].bitcast(I32),
+                )
+
+        def turn_y(i, h, tiles=range(STEP_TILES), per_store=2, vector_tile=None, slot_major=False):
+            if slot_major:
+                order = [(s, t) for t in range(SLOTS) for s in tiles]
+            else:
+                order = [(s, t) for s in tiles for t in range(SLOTS)]
+            banks = {}
+            for s, t in order:
+                if t == 0:
+                    banks[s] = next_bank([P, SLOTS, P])
+                in_late_half = (i, h, LATE_STEPS.start) in y_cols and s * P >= LATE_STEPS.start
+                step0 = LATE_STEPS.start if in_late_half else 0
+                nc.tensor.transpose(
+                    banks[s][:, t, :], y_cols[i, h, step0][:, t, s * P - step0 : (s + 1) * P - step0], ident[:]
+                )
+            for s0 in range(tiles.start, tiles.stop, per_store):
+                y_rows = work.tile([P, per_store, GROUP], F32, name="y_rows%d%d%d" % (i, h, s0), tag="y_rows", bufs=6)
+                for k in range(per_store):
+                    copy_on(s0 + k == vector_tile)(
+                        out=y_rows[:, k, :].rearrange("j (p t) -> j p t", t=SLOTS),
+                        in_=banks[s0 + k][:].rearrange("j t p -> j p t"),
+                    )
+                nc.sync.dma_start(
+                    out=out_0[i, s0 * P : (s0 + per_store) * P, h * GROUP : (h + 1) * GROUP].rearrange(
+                        "(k j) d -> j k d", j=P
+                    ),
                     in_=y_rows[:],
                 )
 
-        def store_scales():
-            for q in range(4):
-                nc.sync.dma_start(
-                    out=out_2[:, 4 * q : 4 * q + 4, :].rearrange("h r m -> r h m").bitcast(I32),
-                    in_=y_sc[32 * q : 32 * q + 4].bitcast(I32),
-                )
-
-        sort_mix(0, 0)
-        sort_mix(1, 0)
-        for n in range(8):
-            horizon(0, n)
-        norm["cols"] = rows_to_columns(norm_rows, 20, "norm_cols")[:].bitcast(BF16)
-        quantise_mix(0, 0)
-        turn_v(0)
-        affine_steps[0]()
-        quantise_mix(1, 0)
-        affine_steps[1]()
-        quantise_v(0, 0)
-        affine_steps[2]()
-        quantise_v(0, 1)
-        affine_steps[3]()
-        horizon(1, 0)
-        horizon(1, 1)
-        sort_mix(0, 1)
-        for i in range(INST - 1):
-            last = i + 2 == INST
+        def first_group_round(i):
             channel_mix(i, 0, 0)
             channel_mix(i, 0, 1)
             horizon(i + 1, 2)
@@ -337,43 +354,82 @@ def tile_revin_horizon_channel_mix_k5_kernel(
             horizon(i + 1, 3)
             if i > 0:
                 quantise_y(i - 1, 1)
-                turn_y(i - 1, 1, ())
+                store_scales(i - 1)
+                turn_y(i - 1, 1)
             else:
                 quantise_mix(0, 1)
                 quantise_mix(1, 1)
-            for n in range(4, 8):
-                horizon(i + 1, n)
+
+        def second_group_round(i):
+            for part in range(4, 8):
+                horizon(i + 1, part)
             channel_mix(i, 1, 0)
             channel_mix(i, 1, 1)
             round_y(i, 0)
             turn_v(i + 1)
             quantise_v(i + 1, 0)
-            channel_mix(i, 1, 2, last)
-            channel_mix(i, 1, 3, last)
+            channel_mix(i, 1, 2)
+            channel_mix(i, 1, 3)
             quantise_v(i + 1, 1)
-            if not last:
-                horizon(i + 2, 0)
-                horizon(i + 2, 1)
+            horizon(i + 2, 0)
+            horizon(i + 2, 1)
             quantise_y(i, 0)
-            turn_y(i, 0, (1,))
-        i = INST - 1
-        early, late = slice(0, HOR // 2), slice(HOR // 2, HOR)
-        channel_mix(i, 0, 0)
-        channel_mix(i, 0, 1, True)
-        round_y(i - 1, 1)
-        channel_mix(i, 0, 2)
-        channel_mix(i, 0, 3)
-        turn_y(i - 1, 1, (1,))
-        quantise_y(i - 1, 1)
-        channel_mix_half(i, 1, early)
-        round_y(i, 0)
-        turn_y(i, 0, ())
-        quantise_y(i, 0)
-        round_y(i, 1, early)
-        channel_mix_half(i, 1, late)
-        quantise_y(i, 1, early)
-        turn_y(i, 1, (), range(0, 2))
-        round_y(i, 1, late)
-        quantise_y(i, 1, late)
-        store_scales()
-        turn_y(i, 1, (3,), range(2, 4), 1)
+            turn_y(i, 0, vector_tile=1)
+
+        sort_mix(0, 0)
+        sort_mix(1, 0)
+        for part in range(CH_GROUPS * STEP_TILES):
+            horizon(0, part)
+        affine = affine_steps(rows_to_columns(norm_rows, NORM_ROWS, "norm_cols")[:].bitcast(BF16))
+        quantise_mix(0, 0)
+        turn_v(0)
+        affine[0]()
+        quantise_mix(1, 0)
+        affine[1]()
+        quantise_v(0, 0)
+        affine[2]()
+        quantise_v(0, 1)
+        affine[3]()
+        horizon(1, 0)
+        horizon(1, 1)
+        sort_mix(0, 1, on_vector=True)
+
+        for i in range(INST - 2):
+            first_group_round(i)
+            second_group_round(i)
+
+        last = INST - 1
+        first_group_round(last - 1)
+        for part in range(4, 7):
+            horizon(last, part)
+        round_y(last - 1, 0)
+        turn_y(last - 1, 0)
+        horizon(last, 7)
+        quantise_y(last - 1, 0)
+        channel_mix(last - 1, 1, 0)
+        channel_mix(last - 1, 1, 1)
+        turn_v(last, shared_copies=True)
+        quantise_v(last, 0)
+        channel_mix(last - 1, 1, 2)
+        channel_mix(last - 1, 1, 3, on_vector=True)
+        quantise_v(last, 1)
+        round_y(last - 1, 1)
+        turn_y(last - 1, 1, slot_major=True)
+        quantise_y(last - 1, 1)
+        store_scales(last - 1)
+
+        for t in range(SLOTS):
+            channel_mix(last, 0, t, on_vector=(t % 2 == 0))
+        round_y(last, 0)
+        channel_mix_half(last, 1, EARLY_STEPS)
+        turn_y(last, 0)
+        quantise_y(last, 0)
+        round_y(last, 1, EARLY_STEPS)
+        channel_mix_half(last, 1, LATE_STEPS)
+        quantise_y(last, 1, EARLY_STEPS)
+        turn_y(last, 1, tiles=range(0, 2))
+        round_y(last, 1, LATE_STEPS)
+        turn_y(last, 1, tiles=range(2, 3), per_store=1)
+        quantise_y(last, 1, LATE_STEPS)
+        turn_y(last, 1, tiles=range(3, 4), per_store=1, vector_tile=3)
+        store_scales(last)

from contextlib import ExitStack

import concourse.mybir as mybir
from concourse.masks import make_identity

INST, LOOK, HOR, CH = 4, 1024, 512, 1024
FLOPS = 2 * INST * HOR * CH * (LOOK + CH)

F32 = mybir.dt.float32
BF16 = mybir.dt.bfloat16
I32 = mybir.dt.int32
U32 = mybir.dt.uint32
U8 = mybir.dt.uint8
FP8X4 = mybir.dt.float8_e4m3fn_x4
FP4X4 = mybir.dt.float4_e2m1fn_x4
ALU = mybir.AluOpType
IDENTITY = mybir.ActivationFunctionType.Identity

P = 128
SLOTS = 4
GROUP = P * SLOTS
LOOK_GROUPS = LOOK // GROUP
CH_GROUPS = CH // GROUP
STEP_TILES = HOR // P
QUADRANTS = 4
FP4_BYTES = 2
BANKS = 8
ALIGN = 64
ALL_STEPS = slice(0, HOR)
EARLY_STEPS, LATE_STEPS = slice(0, HOR // 2), slice(HOR // 2, HOR)
GAMMA_ROW, BETA_ROW, STD_ROW = 0, CH_GROUPS, 2 * CH_GROUPS
MEAN_ROW = STD_ROW + INST * CH_GROUPS
NORM_ROWS = MEAN_ROW + INST * CH_GROUPS


def tile_revin_horizon_channel_mix_k5_kernel(
    tc, x_words, x_scales, a_words, a_scales, bias, gain, mix, gamma, beta, std, mean, out_0, out_1, out_2
):
    nc = tc.nc
    with ExitStack() as ctx:
        keep = ctx.enter_context(tc.tile_pool(name="keep", bufs=1))
        work = ctx.enter_context(tc.tile_pool(name="work", bufs=2))
        psum = ctx.enter_context(tc.psum_pool(name="psum", bufs=1))
        ctx.enter_context(tc.manual_schedule())

        banks_taken = []

        def next_bank(shape):
            count = len(banks_taken)
            banks_taken.append(count)
            return psum.tile(shape, F32, name="bank%d" % count, tag="bank%d" % (count % BANKS))

        def copy_on(vector):
            return nc.vector.tensor_copy if vector else nc.scalar.copy

        a_sc = keep.tile([P, LOOK_GROUPS, HOR], U8, name="a_sc", align_bytes=ALIGN)
        x_sc_first = keep.tile([P, LOOK_GROUPS, CH], U8, name="x_sc_first", align_bytes=ALIGN)
        x_sc_rest = keep.tile([P, LOOK_GROUPS, (INST - 1) * CH], U8, name="x_sc_rest", align_bytes=ALIGN)
        ident = keep.tile([P, P], F32, name="ident")
        gain_rows = keep.tile([P, GROUP // 2], F32, name="gain_rows")
        bias_rows = keep.tile([P, P], F32, name="bias_rows")
        norm_rows = keep.tile([P, GROUP // 2], F32, name="norm_rows")
        nc.vector.memset(gain_rows[:], 0.0)
        nc.vector.memset(a_sc[:].bitcast(I32), 0)
        nc.vector.memset(x_sc_first[:].bitcast(I32), 0)
        nc.vector.memset(bias_rows[:], 0.0)
        nc.vector.memset(norm_rows[:], 0.0)
        nc.vector.memset(x_sc_rest[:].bitcast(I32), 0)

        def load_scales(dst, src):
            for quad in range(QUADRANTS):
                nc.sync.dma_start(
                    out=dst[32 * quad : 32 * quad + 4].bitcast(I32),
                    in_=src[:, 4 * quad : 4 * quad + 4, :].rearrange("n r c -> r n c").bitcast(I32),
                )

        x_w = {}

        def load_x(i, g):
            x_w[i, g] = keep.tile([P, LOOK_GROUPS, FP4_BYTES * GROUP], U8, name="x_w%d%d" % (i, g), align_bytes=ALIGN)
            byte0 = FP4_BYTES * (i * CH + g * GROUP)
            nc.sync.dma_start(
                out=x_w[i, g][:].bitcast(I32),
                in_=x_words[:, :, byte0 : byte0 + FP4_BYTES * GROUP].rearrange("n p b -> p n b").bitcast(I32),
            )

        def load_rows(dst, row0, src):
            nc.sync.dma_start(out=dst[row0 : row0 + src.shape[0], :].bitcast(BF16), in_=src)

        mix_raw = {}

        def load_mix(g, h):
            mix_raw[g, h] = keep.tile([P, SLOTS, GROUP], BF16, name="mix_raw%d%d" % (g, h))
            nc.sync.dma_start(
                out=mix_raw[g, h][:],
                in_=mix[g * GROUP : (g + 1) * GROUP, h * GROUP : (h + 1) * GROUP].rearrange("(p t) d -> p t d", t=SLOTS),
            )

        a_w = keep.tile([P, LOOK_GROUPS, FP4_BYTES * HOR], U8, name="a_w", align_bytes=ALIGN)
        bias_raw = keep.tile([STEP_TILES, P], BF16, name="bias_raw")
        nc.sync.dma_start(out=bias_raw[:], in_=bias.rearrange("(s p) -> s p", p=P))
        load_rows(gain_rows, 0, gain.rearrange("(g c) -> g c", g=CH_GROUPS))
        load_scales(a_sc, a_scales)
        nc.sync.dma_start(out=a_w[:].bitcast(I32), in_=a_words.rearrange("n p b -> p n b").bitcast(I32))
        load_x(0, 0)
        load_scales(x_sc_first, x_scales[:, :, 0:CH])
        make_identity(nc, ident[:])
        load_mix(0, 0)
        load_x(0, 1)
        load_mix(1, 0)
        load_rows(norm_rows, GAMMA_ROW, gamma.rearrange("(h d) -> h d", h=CH_GROUPS))
        load_rows(norm_rows, BETA_ROW, beta.rearrange("(h d) -> h d", h=CH_GROUPS))
        load_rows(norm_rows, STD_ROW, std.rearrange("i (h d) -> (i h) d", h=CH_GROUPS))
        load_rows(norm_rows, MEAN_ROW, mean.rearrange("i (h d) -> (i h) d", h=CH_GROUPS))
        load_scales(x_sc_rest, x_scales[:, :, CH:])
        load_x(1, 0)
        load_mix(0, 1)
        load_mix(1, 1)
        load_x(1, 1)
        for i in range(2, INST):
            for g in range(CH_GROUPS):
                load_x(i, g)

        def rows_to_columns(rows, count, name):
            cols = keep.tile([P, count, 2], F32, name=name)
            bank = next_bank([P, 2, P])
            for u in range(2):
                nc.tensor.transpose(bank[:, u, :], rows[:].rearrange("r (p u) -> r u p", u=2)[:, u, :], ident[:])
            nc.scalar.copy(out=cols[:], in_=bank[:, :, 0:count].rearrange("p u r -> p r u"))
            return cols

        nc.scalar.activation(out=bias_rows[0:STEP_TILES, :], in_=bias_raw[:], func=IDENTITY)
        gain_cols = rows_to_columns(gain_rows, CH_GROUPS, "gain_cols")
        bias_col = keep.tile([P, STEP_TILES], F32, name="bias_col")
        bias_bank = next_bank([P, P])
        nc.tensor.transpose(bias_bank[:], bias_rows[:], ident[:])
        nc.scalar.copy(out=bias_col[:], in_=bias_bank[:, 0:STEP_TILES])
        gain_words = keep.tile([P, CH // 2], F32, name="gain_words")
        gain_bank = next_bank([P, CH_GROUPS, 2, P])
        for g in range(CH_GROUPS):
            for u in range(2):
                nc.tensor.transpose(gain_bank[:, g, u, :], gain_cols[:, g, u : u + 1].to_broadcast([P, P]), ident[:])
        nc.scalar.copy(out=gain_words[:], in_=gain_bank[:].rearrange("p g u w -> p (g u w)"))
        gain_spread = gain_words[:].bitcast(BF16).rearrange("p (g u w e) -> p g u w e", g=CH_GROUPS, u=2, e=2)

        affine_shape = [P, INST, CH_GROUPS * SLOTS]
        slope = keep.tile(affine_shape, F32, name="slope")
        offset = keep.tile(affine_shape, F32, name="offset")
        inv_gamma = keep.tile([P, CH_GROUPS * SLOTS], F32, name="inv_gamma")
        beta_slope = keep.tile(affine_shape, F32, name="beta_slope")

        def affine_steps(norm_cols):
            def per_instance(row0):
                return norm_cols[:, row0 : row0 + INST * CH_GROUPS, :].rearrange("p (i h) t -> p i (h t)", h=CH_GROUPS)

            def shared(row0):
                return norm_cols[:, row0 : row0 + CH_GROUPS, :].rearrange("p h t -> p (h t)")

            return [
                lambda: nc.vector.reciprocal(out=inv_gamma[:], in_=shared(GAMMA_ROW)),
                lambda: nc.vector.tensor_tensor(
                    out=slope[:],
                    in0=per_instance(STD_ROW),
                    in1=inv_gamma[:].unsqueeze(1).to_broadcast(affine_shape),
                    op=ALU.mult,
                ),
                lambda: nc.vector.tensor_tensor(
                    out=beta_slope[:],
                    in0=slope[:],
                    in1=shared(BETA_ROW).unsqueeze(1).to_broadcast(affine_shape),
                    op=ALU.mult,
                ),
                lambda: nc.vector.tensor_tensor(
                    out=offset[:], in0=per_instance(MEAN_ROW), in1=beta_slope[:], op=ALU.subtract
                ),
            ]

        mix_sorted, mix_q, mix_sc = {}, {}, {}

        def sort_mix(g, h, on_vector=False):
            mix_sorted[g, h] = work.tile(
                [P, SLOTS * GROUP], BF16, name="mix_sorted%d%d" % (g, h), tag="mix_sorted", bufs=4, align_bytes=ALIGN
            )
            copy_on(on_vector)(
                out=mix_sorted[g, h][:].rearrange("p (o b m t) -> p b o m t", o=SLOTS, m=2, t=SLOTS),
                in_=mix_raw[g, h][:].rearrange("p t (b m o) -> p b o m t", m=2, o=SLOTS),
            )

        def quantise_mix(g, h):
            mix_q[g, h] = keep.tile([P, GROUP], U32, name="mix_q%d%d" % (g, h), align_bytes=ALIGN)
            mix_sc[g, h] = keep.tile([P, GROUP], U8, name="mix_sc%d%d" % (g, h), align_bytes=ALIGN)
            nc.vector.quantize_mx(out=mix_q[g, h][:].bitcast(FP8X4), scales=mix_sc[g, h][:], in_=mix_sorted[g, h][:])

        v_rows, v_cols, v_q, v_sc = {}, {}, {}, {}

        def horizon(i, part):
            g, s = divmod(part, STEP_TILES)
            bank = next_bank([P, GROUP])
            x_sc, col0 = (x_sc_first, g * GROUP) if i == 0 else (x_sc_rest, (i - 1) * CH + g * GROUP)
            for n in range(LOOK_GROUPS):
                nc.tensor.matmul_mx(
                    out=bank[:],
                    lhsT=a_w[:, n, FP4_BYTES * P * s : FP4_BYTES * P * (s + 1)].bitcast(FP4X4),
                    lhsT_scale=a_sc[:, n, P * s : P * (s + 1)],
                    rhs=x_w[i, g][:, n, :].bitcast(FP4X4),
                    rhs_scale=x_sc[:, n, col0 : col0 + GROUP],
                    start=(n == 0),
                    stop=(n == LOOK_GROUPS - 1),
                )
            v_rows[i, g, s] = work.tile([P, GROUP], BF16, name="v_rows%d%d%d" % (i, g, s), tag="v_rows", bufs=16)
            for u in range(2):
                nc.vector.scalar_tensor_tensor(
                    out=v_rows[i, g, s][:].rearrange("p (u w e) -> p u w e", u=2, e=2)[:, u],
                    in0=bank[:].rearrange("p (w u e) -> p u w e", u=2, e=2)[:, u],
                    scalar=bias_col[:, s : s + 1],
                    in1=gain_spread[:, g, u],
                    op0=ALU.add,
                    op1=ALU.mult,
                )

        def turn_v(i, shared_copies=False):
            for g in range(CH_GROUPS):
                v_cols[i, g] = work.tile(
                    [P, HOR * 2], F32, name="v_cols%d%d" % (i, g), tag="v_cols", bufs=3, align_bytes=ALIGN
                )
                for half in range(2):
                    bank = next_bank([P, 2, 2, P])
                    for k in range(2):
                        words = v_rows[i, g, 2 * half + k][:].bitcast(F32)
                        for u in range(2):
                            nc.tensor.transpose(bank[:, k, u, :], words[:, u * P : (u + 1) * P], ident[:])
                    copy_on(shared_copies and half == 1)(
                        out=v_cols[i, g][:, half * HOR : (half + 1) * HOR].rearrange("p (k j u) -> p k j u", k=2, u=2),
                        in_=bank[:].rearrange("p k u j -> p k j u"),
                    )

        def quantise_v(i, g):
            v_q[i, g] = work.tile([P, HOR], U32, name="v_q%d%d" % (i, g), tag="v_q", bufs=4, align_bytes=ALIGN)
            v_sc[i, g] = work.tile([P, HOR], U8, name="v_sc%d%d" % (i, g), tag="v_sc", bufs=4, align_bytes=ALIGN)
            nc.vector.quantize_mx(
                out=v_q[i, g][:].bitcast(FP8X4), scales=v_sc[i, g][:], in_=v_cols[i, g][:].bitcast(BF16)
            )

        y_cols, y_bf, y_q = {}, {}, {}
        y_sc = [keep.tile([P, CH_GROUPS, HOR], U8, name="y_sc%d" % i, align_bytes=ALIGN) for i in range(INST)]

        def mix_passes(sums, i, h, t, steps):
            for g in range(CH_GROUPS):
                nc.tensor.matmul_mx(
                    out=sums,
                    lhsT=mix_q[g, h][:, P * t : P * (t + 1)].bitcast(FP8X4),
                    lhsT_scale=mix_sc[g, h][:, P * t : P * (t + 1)],
                    rhs=v_q[i, g][:, steps].bitcast(FP8X4),
                    rhs_scale=v_sc[i, g][:, steps],
                    start=(g == 0),
                    stop=(g == CH_GROUPS - 1),
                )

        def denormalise(sums, i, h, t, steps, on_vector):
            key = (i, h, steps.start)
            if key not in y_cols:
                y_cols[key] = work.tile(
                    [P, SLOTS, steps.stop - steps.start], F32, name="y_cols%d%d%d" % key, tag="y_cols", bufs=4
                )
            slope_col = slope[:, i, h * SLOTS + t : h * SLOTS + t + 1]
            offset_col = offset[:, i, h * SLOTS + t : h * SLOTS + t + 1]
            if on_vector:
                nc.vector.tensor_scalar(
                    out=y_cols[key][:, t, :], in0=sums, scalar1=slope_col, scalar2=offset_col, op0=ALU.mult, op1=ALU.add
                )
            else:
                nc.scalar.activation(out=y_cols[key][:, t, :], in_=sums, func=IDENTITY, scale=slope_col, bias=offset_col)

        def channel_mix(i, h, t, on_vector=False):
            bank = next_bank([P, HOR])
            mix_passes(bank[:], i, h, t, ALL_STEPS)
            denormalise(bank[:], i, h, t, ALL_STEPS, on_vector)

        def channel_mix_half(i, h, steps):
            for t0 in (0, 2):
                bank = next_bank([P, 2, HOR // 2])
                for k in range(2):
                    mix_passes(bank[:, k, :], i, h, t0 + k, steps)
                for k in range(2):
                    denormalise(bank[:, k, :], i, h, t0 + k, steps, on_vector=(t0 == 2))

        def round_y(i, h, steps=ALL_STEPS):
            key = (i, h, steps.start)
            y_bf[key] = work.tile(
                [P, (steps.stop - steps.start) * SLOTS], BF16, name="y_bf%d%d%d" % key, tag="y_bf", align_bytes=ALIGN
            )
            nc.vector.tensor_copy(
                out=y_bf[key][:].rearrange("p (b r t) -> p b t r", r=4, t=SLOTS),
                in_=y_cols[key][:].rearrange("p t (b r) -> p b t r", r=4),
            )

        def quantise_y(i, h, steps=ALL_STEPS):
            if steps.start == 0:
                y_q[i, h] = work.tile([P, HOR], U32, name="y_q%d%d" % (i, h), tag="y_q", bufs=3, align_bytes=ALIGN)
            nc.vector.quantize_mx(
                out=y_q[i, h][:, steps].bitcast(FP8X4), scales=y_sc[i][:, h, steps], in_=y_bf[i, h, steps.start][:]
            )
            if steps.stop == HOR:
                nc.sync.dma_start(
                    out=out_1[h, :, i * HOR : (i + 1) * HOR, :].rearrange("p j t -> p (j t)").bitcast(I32),
                    in_=y_q[i, h][:].bitcast(I32),
                )

        def store_scales(i):
            for quad in range(QUADRANTS):
                nc.sync.dma_start(
                    out=out_2[:, 4 * quad : 4 * quad + 4, i * HOR : (i + 1) * HOR].rearrange("h r j -> r h j").bitcast(I32),
                    in_=y_sc[i][32 * quad : 32 * quad + 4].bitcast(I32),
                )

        def turn_y(i, h, tiles=range(STEP_TILES), per_store=2, vector_tile=None, slot_major=False):
            if slot_major:
                order = [(s, t) for t in range(SLOTS) for s in tiles]
            else:
                order = [(s, t) for s in tiles for t in range(SLOTS)]
            banks = {}
            for s, t in order:
                if t == 0:
                    banks[s] = next_bank([P, SLOTS, P])
                in_late_half = (i, h, LATE_STEPS.start) in y_cols and s * P >= LATE_STEPS.start
                step0 = LATE_STEPS.start if in_late_half else 0
                nc.tensor.transpose(
                    banks[s][:, t, :], y_cols[i, h, step0][:, t, s * P - step0 : (s + 1) * P - step0], ident[:]
                )
            for s0 in range(tiles.start, tiles.stop, per_store):
                y_rows = work.tile([P, per_store, GROUP], F32, name="y_rows%d%d%d" % (i, h, s0), tag="y_rows", bufs=6)
                for k in range(per_store):
                    copy_on(s0 + k == vector_tile)(
                        out=y_rows[:, k, :].rearrange("j (p t) -> j p t", t=SLOTS),
                        in_=banks[s0 + k][:].rearrange("j t p -> j p t"),
                    )
                nc.sync.dma_start(
                    out=out_0[i, s0 * P : (s0 + per_store) * P, h * GROUP : (h + 1) * GROUP].rearrange(
                        "(k j) d -> j k d", j=P
                    ),
                    in_=y_rows[:],
                )

        def first_group_round(i):
            channel_mix(i, 0, 0)
            channel_mix(i, 0, 1)
            horizon(i + 1, 2)
            if i > 0:
                round_y(i - 1, 1)
            else:
                sort_mix(1, 1)
            channel_mix(i, 0, 2)
            channel_mix(i, 0, 3)
            horizon(i + 1, 3)
            if i > 0:
                quantise_y(i - 1, 1)
                store_scales(i - 1)
                turn_y(i - 1, 1)
            else:
                quantise_mix(0, 1)
                quantise_mix(1, 1)

        def second_group_round(i):
            for part in range(4, 8):
                horizon(i + 1, part)
            channel_mix(i, 1, 0)
            channel_mix(i, 1, 1)
            round_y(i, 0)
            turn_v(i + 1)
            quantise_v(i + 1, 0)
            channel_mix(i, 1, 2)
            channel_mix(i, 1, 3)
            quantise_v(i + 1, 1)
            horizon(i + 2, 0)
            horizon(i + 2, 1)
            quantise_y(i, 0)
            turn_y(i, 0, vector_tile=1)

        sort_mix(0, 0)
        sort_mix(1, 0)
        for part in range(CH_GROUPS * STEP_TILES):
            horizon(0, part)
        affine = affine_steps(rows_to_columns(norm_rows, NORM_ROWS, "norm_cols")[:].bitcast(BF16))
        quantise_mix(0, 0)
        turn_v(0)
        affine[0]()
        quantise_mix(1, 0)
        affine[1]()
        quantise_v(0, 0)
        affine[2]()
        quantise_v(0, 1)
        affine[3]()
        horizon(1, 0)
        horizon(1, 1)
        sort_mix(0, 1, on_vector=True)

        for i in range(INST - 2):
            first_group_round(i)
            second_group_round(i)

        last = INST - 1
        first_group_round(last - 1)
        for part in range(4, 7):
            horizon(last, part)
        round_y(last - 1, 0)
        turn_y(last - 1, 0)
        horizon(last, 7)
        quantise_y(last - 1, 0)
        channel_mix(last - 1, 1, 0)
        channel_mix(last - 1, 1, 1)
        turn_v(last, shared_copies=True)
        quantise_v(last, 0)
        channel_mix(last - 1, 1, 2)
        channel_mix(last - 1, 1, 3, on_vector=True)
        quantise_v(last, 1)
        round_y(last - 1, 1)
        turn_y(last - 1, 1, slot_major=True)
        quantise_y(last - 1, 1)
        store_scales(last - 1)

        for t in range(SLOTS):
            channel_mix(last, 0, t, on_vector=(t % 2 == 0))
        round_y(last, 0)
        channel_mix_half(last, 1, EARLY_STEPS)
        turn_y(last, 0)
        quantise_y(last, 0)
        round_y(last, 1, EARLY_STEPS)
        channel_mix_half(last, 1, LATE_STEPS)
        quantise_y(last, 1, EARLY_STEPS)
        turn_y(last, 1, tiles=range(0, 2))
        round_y(last, 1, LATE_STEPS)
        turn_y(last, 1, tiles=range(2, 3), per_store=1)
        quantise_y(last, 1, LATE_STEPS)
        turn_y(last, 1, tiles=range(3, 4), per_store=1, vector_tile=3)
        store_scales(last)
